import numpy as np
import ml_dtypes


def mxq(x, axis, fmt="e4m3"):
    dtype, down = {"e4m3": (ml_dtypes.float8_e4m3fn, 7), "e5m2": (ml_dtypes.float8_e5m2, 14)}[fmt]
    v = np.moveaxis(np.asarray(x, np.float32).astype(ml_dtypes.bfloat16).astype(np.float64), axis, -1)
    blocks = v.reshape(v.shape[:-1] + (-1, 32))
    amax = np.abs(blocks).max(-1, keepdims=True)
    byte = np.maximum(np.where(amax > 0, np.frexp(amax)[1] - 1 + 127, 0) - down, 1)
    scale = np.exp2(byte - 127.0)
    codes = (blocks / scale).astype(np.float32).astype(dtype).astype(np.float64)
    return np.moveaxis((codes * scale).reshape(v.shape), -1, axis)


WIDE = False


def mx_kscale(k):
    if not WIDE:
        return np.ones(k)
    levels = np.array([10, -10, 5, -5, 0])
    if k % 512:
        return np.exp2(np.random.permutation(np.resize(levels, k // 32))).repeat(32)
    a = np.empty((k // 512, 16))
    for p in range(k // 512):
        a[p, :8] = np.random.permutation(np.resize(levels, 8))
        for g in range(8):
            far = levels[np.abs(levels - a[p, g]) >= 10]
            a[p, g + 8] = far[np.random.randint(len(far))]
    return np.exp2(a.ravel()).repeat(32)


def f64(x):
    return np.asarray(x).astype(np.float64)


def striped(idx):
    return np.tile(np.asarray(idx).reshape(-1, 16).T, (8, 1)).astype(np.uint16)


def unstriped(offs):
    return offs[:16].T.reshape(-1).astype(np.int64)


E2M1 = np.array([0.0, 0.5, 1.0, 1.5, 2.0, 3.0, 4.0, 6.0, -0.0, -0.5, -1.0, -1.5, -2.0, -3.0, -4.0, -6.0])


def pack_weight(w, fmt):
    k, n = w.shape
    w = f64(np.asarray(w, np.float32).astype(ml_dtypes.bfloat16)).reshape(k // 32, 32, n)
    amax = np.abs(w).max(1)
    if fmt == "e4m3":
        byte = np.frexp(amax)[1] - 1 + 127 - 7
    else:
        mant, ex = np.frexp(amax / 6.0)
        byte = np.where(mant > 0.5, ex, ex - 1) + 127
    byte = np.clip(np.where(amax > 0, byte, 1), 1, 254)
    scaled = (w * np.exp2(127.0 - byte)[:, None, :]).reshape(k, n).astype(np.float32)
    by_word = np.ascontiguousarray(scaled.reshape(k // 512, 128, 4, n).transpose(0, 1, 3, 2))
    if fmt == "e4m3":
        words = by_word.astype(ml_dtypes.float8_e4m3fn).view(np.uint8)
    else:
        c = by_word.astype(ml_dtypes.float4_e2m1fn).view(np.uint8) & 0xF
        words = (c[..., 0::2] | (c[..., 1::2] << 4)).reshape(k // 512, 128, 2 * n)
    return np.ascontiguousarray(words), np.ascontiguousarray(byte.astype(np.uint8).reshape(k // 512, 16, n))


def unpack_weight(words, scales, fmt):
    g, _, n = scales.shape
    words = np.ascontiguousarray(words).reshape(g, 128, n, -1)
    if fmt == "e4m3":
        vals = words.view(ml_dtypes.float8_e4m3fn).astype(np.float64)
    else:
        nib = np.empty((g, 128, n, 4), np.uint8)
        nib[..., 0::2] = words & 0xF
        nib[..., 1::2] = words >> 4
        vals = E2M1[nib]
    vals = vals * np.repeat(np.exp2(scales.astype(np.float64) - 127.0), 8, axis=1)[..., None]
    return vals.transpose(0, 1, 3, 2).reshape(g * 512, n)


D, E, T, I, Q, G = 512, 512, 2048, 512, 128, 32


def setup_inputs():
    n = np.random.standard_normal
    idx = np.random.permutation(T)[:I]
    fd = mx_kscale(D)
    fe = mx_kscale(E)
    keysp = pack_weight(n((D, T)) / fd[:, None], "e2m1")
    valsp = pack_weight(n((E, T)) / fe[:, None], "e2m1")
    return {
        "query": (n((D, Q)) * 0.7 / np.sqrt(D) * fd[:, None]).astype(np.float32),
        "keys_words": keysp[0],
        "keys_scales": keysp[1],
        "temper": (np.random.uniform(0.3, 3.0, (Q, 1))).astype(np.float32),
        "gout": (n((E, Q)) * 1 / np.sqrt(E) * fe[:, None]).astype(np.float32),
        "vals_words": valsp[0],
        "vals_scales": valsp[1],
        "size": (np.random.uniform(0.5, 2.0, (1, I))).astype(np.float32),
        "dquery": (n((D, Q)) * 1.0 / np.sqrt(D) * fd[:, None]).astype(np.float32),
        "base": (0.5 * n((Q, T))).astype(np.float32),
        "offs": striped(idx),
    }


def reference(query, keys_words, keys_scales, temper, gout, vals_words, vals_scales, size, dquery, base, offs):
    idx = unstriped(offs)
    keysu = unpack_weight(keys_words, keys_scales, "e2m1")
    valsu = unpack_weight(vals_words, vals_scales, "e2m1")
    queryq = mxq(f64(query), 0, "e4m3")
    keysidxg = keysu[:, idx]
    a = queryq.T @ keysidxg
    dqueryq = mxq(f64(dquery), 0, "e4m3")
    ta = dqueryq.T @ keysidxg
    x1 = np.exp(a)
    s = x1.reshape(Q, G, I // G).sum(axis=2)
    p = np.exp(np.log(s) * f64(temper))
    z = np.sum(p, axis=1, keepdims=True)
    sh = p / s / z
    sr = np.repeat(sh, I // G, axis=1)
    goutq = mxq(f64(gout), 0, "e4m3")
    valsidxg = valsu[:, idx]
    c0 = goutq.T @ valsidxg
    dsr = c0 * f64(size) * x1
    dsh = dsr.reshape(Q, G, I // G).sum(axis=2)
    dz = np.sum(dsh * p / s / np.square(z) * (-1.0), axis=1, keepdims=True)
    dp = dsh / z / s + dz
    ds = dp * p * f64(temper) / s - dsh / z * p / np.square(s)
    r1 = np.repeat(ds, I // G, axis=1)
    dx1 = c0 * f64(size) * sr + r1
    tx1 = ta * x1
    ts = tx1.reshape(Q, G, I // G).sum(axis=2)
    tp = ts / s * f64(temper) * p
    tz = np.sum(tp, axis=1, keepdims=True)
    tsh = ((tp - ts * p / s) / s - tz * p / s / z) / z
    tsr = np.repeat(tsh, I // G, axis=1)
    tdsr = tx1 * c0 * f64(size)
    tdsh = tdsr.reshape(Q, G, I // G).sum(axis=2)
    tdz = np.sum((tdsh * p / s + (tp - ts * p / s) / s * dsh - tz * z * 2.0 * dsh * p / s / np.square(z)) / np.square(z) * (-1.0), axis=1, keepdims=True)
    tdp = ((tdsh - tz * dsh / z) / z - ts * dsh / z / s) / s + tdz
    tds = ((tdp * p + tp * dp) * f64(temper) - ts * dp * p * f64(temper) / s) / s - ((tdsh - tz * dsh / z) / z * p + tp * dsh / z - ts * s * 2.0 * dsh / z * p / np.square(s)) / np.square(s)
    tr1 = np.repeat(tds, I // G, axis=1)
    tdx1 = tsr * c0 * f64(size) + tr1
    tda = tdx1 * x1 + tx1 * dx1
    gs = tda * 512.0
    gf = np.zeros((Q, T))
    gf[:, idx] = gs
    y = f64(base) + gf
    return y

@@ -1,0 +1,218 @@
+from contextlib import ExitStack
+
+import concourse.mybir as mybir
+
+D, T, I, Q, G = 512, 2048, 512, 128, 32
+P = 128
+PACK = 4
+PAGE = I // G
+FLOPS = 3 * 2 * D * Q * I
+
+F32 = mybir.dt.float32
+BF16 = mybir.dt.bfloat16
+I32 = mybir.dt.int32
+U32 = mybir.dt.uint32
+U16 = mybir.dt.uint16
+U8 = mybir.dt.uint8
+FP8X4 = mybir.dt.float8_e4m3fn_x4
+FP4X4 = mybir.dt.float4_e2m1fn_x4
+ALU = mybir.AluOpType
+ACT = mybir.ActivationFunctionType
+AX = mybir.AxisListType
+
+OUT_SCALE = 512.0
+LN_FLOOR = 2.0 ** -64
+STORE_WIDTHS = (512, 512, 512, 512)
+
+
+def tile_attend_hvtemperedpages_s_kernel(tc, query, keys_words, keys_scales, temper, gout, vals_words, vals_scales, size, dquery, base, offs, out):
+    nc = tc.nc
+    mult, add, sub = ALU.mult, ALU.add, ALU.subtract
+
+    with ExitStack() as ctx:
+        sb = ctx.enter_context(tc.tile_pool(name="sb", bufs=1))
+        ps = ctx.enter_context(tc.psum_pool(name="ps", bufs=1))
+
+        def wide(name):
+            return sb.tile([P, I], F32, name=name)
+
+        def pages(name):
+            return sb.tile([P, G], F32, name=name)
+
+        def column(name):
+            return sb.tile([P, 1], F32, name=name)
+
+        def by_page(t):
+            return t[:].rearrange("p (g j) -> p g j", j=PAGE)
+
+        def spread(t):
+            return t[:].unsqueeze(2).to_broadcast([P, G, PAGE])
+
+        def load_scales(clearer, queue, name, scales):
+            pool_scales = sb.tile([P, T], U8, name=name, tag=name, align_bytes=64)
+            clearer.memset(pool_scales[:].bitcast(I32), 0)
+            rows = scales[0].rearrange("(q r) n -> r q n", r=PACK)
+            for r in range(PACK):
+                queue.dma_start(out=pool_scales[r:P:32, :].bitcast(I32), in_=rows[r].bitcast(I32))
+            return pool_scales
+
+        def load_words(name, words):
+            pool_words = sb.tile([P, T], U16, name=name, tag=name, align_bytes=64)
+            nc.sync.dma_start(out=pool_words[:].bitcast(I32), in_=words[0].bitcast(I32))
+            return pool_words
+
+        def load_rows(name, rows, tag):
+            raw = sb.tile([P, PACK, Q], F32, name=name, tag=tag)
+            nc.sync.dma_start(out=raw[:], in_=rows.rearrange("(p j) w -> p j w", j=PACK))
+            return raw
+
+        def interleave(name, raw):
+            grouped = sb.tile([P, Q, PACK], BF16, name=name, align_bytes=64)
+            nc.scalar.copy(out=grouped[:], in_=raw[:].rearrange("p j w -> p w j"))
+            return grouped
+
+        def quantise(name, grouped):
+            codes = sb.tile([P, Q], U32, name=name + "_codes", align_bytes=64)
+            scales = sb.tile([P, Q], U8, name=name + "_scales", align_bytes=64)
+            nc.vector.quantize_mx(out=codes[:].bitcast(FP8X4), scales=scales[:], in_=grouped[:].rearrange("p w j -> p (w j)"))
+            return codes, scales
+
+        def gather(name, pool_tile, dtype, tag):
+            picked = sb.tile([P, I], dtype, name=name, tag=tag, align_bytes=64)
+            nc.vector.tensor_copy(out=picked[:], in_=pool_tile[:].indirect(offsets[:]))
+            return picked
+
+        def product(name, rows, words, scales):
+            acc = ps.tile([P, I], F32, name=name)
+            nc.tensor.matmul_mx(out=acc[:], lhsT=rows[0][:].bitcast(FP8X4), lhsT_scale=rows[1][:], rhs=words[:].bitcast(FP4X4), rhs_scale=scales[:], start=True, stop=True)
+            return acc
+
+        def page_sum(name, t):
+            total = pages(name)
+            nc.vector.tensor_reduce(out=total[:], in_=by_page(t), axis=AX.X, op=add)
+            return total
+
+        offsets = sb.tile([P, I // 16], U16, name="offsets")
+        nc.sync.dma_start(offsets[:], offs)
+        key_word_pool = load_words("key_word_pool", keys_words)
+        key_scale_pool = load_scales(nc.vector, nc.scalar, "key_scale_pool", keys_scales)
+        query_raw = load_rows("query_raw", query, "query_raw")
+        val_word_pool = load_words("val_word_pool", vals_words)
+        val_scale_pool = load_scales(nc.gpsimd, nc.gpsimd, "val_scale_pool", vals_scales)
+        warm_in = sb.tile([P, 1], F32, name="warm_in", tag="dquery_raw")
+        nc.vector.memset(warm_in[:], 0.0)
+        warm_out = sb.tile([P, 1], F32, name="warm_out", tag="gout_raw")
+        nc.scalar.activation(out=warm_out[:], in_=warm_in[:], func=ACT.Exp)
+        dquery_raw = load_rows("dquery_raw", dquery, "dquery_raw")
+        gout_raw = load_rows("gout_raw", gout, "gout_raw")
+
+        placed = sb.tile([P, T], F32, name="placed")
+        for start in range(0, T, I):
+            nc.vector.memset(placed[:, start : start + I], 0.0)
+
+        key_words = gather("key_words", key_word_pool, U16, "key_words")
+        tau = sb.tile([P, 1], F32, name="tau", tag="key_word_pool", align_bytes=64)
+        nc.sync.dma_start(out=tau[:], in_=temper)
+        tau_less_1 = column("tau_less_1")
+        nc.gpsimd.tensor_scalar(tau_less_1[:], tau[:], 1.0, -1.0, mult, add)
+        neg_tau = column("neg_tau")
+        nc.gpsimd.tensor_scalar(neg_tau[:], tau[:], -1.0, 0.0, mult, add)
+        neg_tau_unscaled = column("neg_tau_unscaled")
+        nc.gpsimd.tensor_scalar(neg_tau_unscaled[:], tau[:], -1.0 / OUT_SCALE, 0.0, mult, add)
+
+        query_mx = quantise("query", interleave("query_bf", query_raw))
+        size_rows = sb.tile([P, I], F32, name="size_rows", tag="query_raw")
+        nc.sync.dma_start(out=size_rows[:], in_=size[0].partition_broadcast(P))
+        key_scales = gather("key_scales", key_scale_pool, U8, "key_scales")
+        a = product("a", query_mx, key_words, key_scales)
+        val_words = gather("val_words", val_word_pool, U16, "key_scale_pool")
+        neg_max = column("neg_max")
+        neg_a = sb.tile([P, I], F32, name="neg_a", tag="val_word_pool", align_bytes=64)
+        nc.vector.tensor_scalar(neg_a[:], a[:], -1.0, None, mult, ALU.min, accum_out=neg_max[:])
+        x = wide("x")
+        nc.scalar.activation(out=x[:], in_=a[:], func=ACT.Exp, bias=neg_max[:], scale=1.0)
+        dquery_mx = quantise("dquery", interleave("dquery_bf", dquery_raw))
+        v = product("v", dquery_mx, key_words, key_scales)
+        gout_mx = quantise("gout", interleave("gout_bf", gout_raw))
+        val_scales = gather("val_scales", val_scale_pool, U8, "val_word_pool")
+        c0 = product("c0", gout_mx, val_words, val_scales)
+        result = sb.tile([P, T], F32, name="result", tag="val_word_pool", align_bytes=64)
+        nc.sync.dma_start(out=result[:], in_=base)
+
+        s = page_sum("s", x)
+        ln_s = pages("ln_s")
+        nc.scalar.activation(out=ln_s[:], in_=s[:], func=ACT.Ln, bias=LN_FLOOR, scale=1.0)
+        p = pages("p")
+        z = column("z")
+        nc.scalar.activation(out=p[:], in_=ln_s[:], func=ACT.Exp, scale=tau[:], accum_out=z[:])
+        pr = pages("pr")
+        nc.scalar.activation(out=pr[:], in_=ln_s[:], func=ACT.Exp, scale=tau_less_1[:])
+        r = pages("r")
+        nc.scalar.activation(out=r[:], in_=ln_s[:], func=ACT.Exp, scale=-1.0)
+
+        xv = wide("xv")
+        nc.vector.tensor_tensor(xv[:], v[:], x[:], mult)
+        ts = page_sum("ts", xv)
+        c = wide("c")
+        nc.vector.tensor_tensor(c[:], c0[:], size_rows[:], mult)
+        xc = wide("xc")
+        nc.vector.tensor_tensor(xc[:], x[:], c[:], mult)
+        dsh = page_sum("dsh", xc)
+
+        rz = column("rz")
+        nc.vector.reciprocal(rz[:], z[:])
+        sums = sb.tile([P, 2], F32, name="sums")
+        terms_m = pages("terms_m")
+        nc.vector.scalar_tensor_tensor(terms_m[:], pr[:], neg_tau[:], dsh[:], mult, mult, accum_out=sums[:, 1:2])
+        terms_v = pages("terms_v")
+        nc.vector.scalar_tensor_tensor(terms_v[:], pr[:], neg_tau[:], ts[:], mult, mult, accum_out=sums[:, 0:1])
+        b = pages("b")
+        nc.vector.scalar_tensor_tensor(b[:], dsh[:], tau_less_1[:], r[:], mult, mult)
+        w = pages("w")
+        nc.vector.tensor_scalar(w[:], pr[:], rz[:], OUT_SCALE, mult, mult)
+        shifts = sb.tile([P, 2], F32, name="shifts")
+        nc.vector.tensor_scalar(shifts[:], sums[:], rz[:], None, mult)
+        av = pages("av")
+        nc.vector.scalar_tensor_tensor(av[:], ts[:], tau_less_1[:], r[:], mult, mult)
+        wb = pages("wb")
+        nc.vector.scalar_tensor_tensor(wb[:], b[:], shifts[:, 1:2], w[:], add, mult)
+
+        t2 = wide("t2")
+        for g in range(G):
+            cols = slice(g * PAGE, (g + 1) * PAGE)
+            nc.scalar.activation(out=t2[:, cols], in_=c[:, cols], func=ACT.Identity, scale=w[:, g : g + 1], bias=wb[:, g : g + 1])
+
+        xvc = wide("xvc")
+        nc.vector.tensor_tensor(xvc[:], xv[:], c[:], mult)
+        ad = pages("ad")
+        nc.vector.tensor_tensor(ad[:], av[:], dsh[:], mult)
+        tdsh = page_sum("tdsh", xvc)
+        t1 = wide("t1")
+        nc.vector.scalar_tensor_tensor(by_page(t1), by_page(v), shifts[:, 0:1], spread(av), add, add)
+
+        y1 = pages("y1")
+        nc.vector.tensor_tensor(y1[:], ad[:], tdsh[:], add)
+        y2 = pages("y2")
+        nc.vector.scalar_tensor_tensor(y2[:], tdsh[:], tau_less_1[:], ad[:], mult, sub)
+        terms_k = pages("terms_k")
+        acc = column("acc")
+        nc.vector.scalar_tensor_tensor(terms_k[:], w[:], neg_tau_unscaled[:], y1[:], mult, mult, accum_out=acc[:])
+        gl = pages("gl")
+        nc.vector.tensor_tensor(gl[:], y2[:], r[:], mult)
+        kappa = column("kappa")
+        nc.vector.tensor_scalar(kappa[:], shifts[:, 0:1], shifts[:, 1:2], acc[:], mult, add)
+        wc = pages("wc")
+        nc.vector.scalar_tensor_tensor(wc[:], gl[:], kappa[:], w[:], add, mult)
+
+        t3 = wide("t3")
+        nc.vector.tensor_tensor(t3[:], t1[:], t2[:], mult)
+        t4 = wide("t4")
+        nc.vector.tensor_tensor(by_page(t4), by_page(t3), spread(wc), add)
+        nc.vector.tensor_tensor(placed[:].indirect(offsets[:]), t4[:], x[:], mult)
+
+        start = 0
+        for n, width in enumerate(STORE_WIDTHS):
+            cols = slice(start, start + width)
+            nc.vector.tensor_tensor(result[:, cols], result[:, cols], placed[:, cols], add)
+            (nc.sync if n % 2 == 0 else nc.scalar).dma_start(out=out[:, cols], in_=result[:, cols])
+            start += width

@@ -22,7 +22,7 @@ AX = mybir.AxisListType
 
 OUT_SCALE = 512.0
 LN_FLOOR = 2.0 ** -64
-STORE_WIDTHS = (512, 512, 512, 512)
+STORE_WIDTHS = (384, 512, 512, 448, 192)
 
 
 def tile_attend_hvtemperedpages_s_kernel(tc, query, keys_words, keys_scales, temper, gout, vals_words, vals_scales, size, dquery, base, offs, out):
@@ -33,11 +33,11 @@ def tile_attend_hvtemperedpages_s_kernel(tc, query, keys_words, keys_scales, tem
         sb = ctx.enter_context(tc.tile_pool(name="sb", bufs=1))
         ps = ctx.enter_context(tc.psum_pool(name="ps", bufs=1))
 
-        def wide(name):
-            return sb.tile([P, I], F32, name=name)
+        def wide(name, tag=None):
+            return sb.tile([P, I], F32, name=name, tag=tag or name)
 
-        def pages(name):
-            return sb.tile([P, G], F32, name=name)
+        def pages(name, tag=None):
+            return sb.tile([P, G], F32, name=name, tag=tag or name, align_bytes=64)
 
         def column(name):
             return sb.tile([P, 1], F32, name=name)
@@ -66,16 +66,18 @@ def tile_attend_hvtemperedpages_s_kernel(tc, query, keys_words, keys_scales, tem
             nc.sync.dma_start(out=raw[:], in_=rows.rearrange("(p j) w -> p j w", j=PACK))
             return raw
 
-        def interleave(name, raw):
-            grouped = sb.tile([P, Q, PACK], BF16, name=name, align_bytes=64)
-            nc.scalar.copy(out=grouped[:], in_=raw[:].rearrange("p j w -> p w j"))
+        def interleave(name, raws):
+            grouped = sb.tile([P, len(raws) * Q, PACK], BF16, name=name, align_bytes=64)
+            for n, raw in enumerate(raws):
+                nc.scalar.copy(out=grouped[:, n * Q : (n + 1) * Q, :], in_=raw[:].rearrange("p j w -> p w j"))
             return grouped
 
         def quantise(name, grouped):
-            codes = sb.tile([P, Q], U32, name=name + "_codes", align_bytes=64)
-            scales = sb.tile([P, Q], U8, name=name + "_scales", align_bytes=64)
+            width = grouped.shape[1]
+            codes = sb.tile([P, width], U32, name=name + "_codes", align_bytes=64)
+            scales = sb.tile([P, width], U8, name=name + "_scales", align_bytes=64)
             nc.vector.quantize_mx(out=codes[:].bitcast(FP8X4), scales=scales[:], in_=grouped[:].rearrange("p w j -> p (w j)"))
-            return codes, scales
+            return [(codes[:, n : n + Q], scales[:, n : n + Q]) for n in range(0, width, Q)]
 
         def gather(name, pool_tile, dtype, tag):
             picked = sb.tile([P, I], dtype, name=name, tag=tag, align_bytes=64)
@@ -84,7 +86,7 @@ def tile_attend_hvtemperedpages_s_kernel(tc, query, keys_words, keys_scales, tem
 
         def product(name, rows, words, scales):
             acc = ps.tile([P, I], F32, name=name)
-            nc.tensor.matmul_mx(out=acc[:], lhsT=rows[0][:].bitcast(FP8X4), lhsT_scale=rows[1][:], rhs=words[:].bitcast(FP4X4), rhs_scale=scales[:], start=True, stop=True)
+            nc.tensor.matmul_mx(out=acc[:], lhsT=rows[0].bitcast(FP8X4), lhsT_scale=rows[1], rhs=words[:].bitcast(FP4X4), rhs_scale=scales[:], start=True, stop=True)
             return acc
 
         def page_sum(name, t):
@@ -95,51 +97,53 @@ def tile_attend_hvtemperedpages_s_kernel(tc, query, keys_words, keys_scales, tem
         offsets = sb.tile([P, I // 16], U16, name="offsets")
         nc.sync.dma_start(offsets[:], offs)
         key_word_pool = load_words("key_word_pool", keys_words)
-        key_scale_pool = load_scales(nc.vector, nc.scalar, "key_scale_pool", keys_scales)
+        key_scale_pool = load_scales(nc.vector, nc.sync, "key_scale_pool", keys_scales)
         query_raw = load_rows("query_raw", query, "query_raw")
-        val_word_pool = load_words("val_word_pool", vals_words)
-        val_scale_pool = load_scales(nc.gpsimd, nc.gpsimd, "val_scale_pool", vals_scales)
         warm_in = sb.tile([P, 1], F32, name="warm_in", tag="dquery_raw")
-        nc.vector.memset(warm_in[:], 0.0)
+        warm_bias = sb.tile([P, 1], F32, name="warm_bias", tag="val_word_pool", align_bytes=64)
+        warm_scale = sb.tile([P, 1], F32, name="warm_scale", tag="val_scale_pool", align_bytes=64)
+        for operand in (warm_in, warm_bias, warm_scale):
+            nc.gpsimd.memset(operand[:], 0.0)
         warm_out = sb.tile([P, 1], F32, name="warm_out", tag="gout_raw")
-        nc.scalar.activation(out=warm_out[:], in_=warm_in[:], func=ACT.Exp)
+        nc.scalar.activation(out=warm_out[:], in_=warm_in[:], func=ACT.Exp, bias=warm_bias[:], scale=warm_scale[:])
+        val_word_pool = load_words("val_word_pool", vals_words)
         dquery_raw = load_rows("dquery_raw", dquery, "dquery_raw")
         gout_raw = load_rows("gout_raw", gout, "gout_raw")
 
         placed = sb.tile([P, T], F32, name="placed")
-        for start in range(0, T, I):
-            nc.vector.memset(placed[:, start : start + I], 0.0)
+        nc.vector.memset(placed[:], 0.0)
+        val_scale_pool = load_scales(nc.vector, nc.sync, "val_scale_pool", vals_scales)
 
         key_words = gather("key_words", key_word_pool, U16, "key_words")
         tau = sb.tile([P, 1], F32, name="tau", tag="key_word_pool", align_bytes=64)
         nc.sync.dma_start(out=tau[:], in_=temper)
         tau_less_1 = column("tau_less_1")
         nc.gpsimd.tensor_scalar(tau_less_1[:], tau[:], 1.0, -1.0, mult, add)
-        neg_tau = column("neg_tau")
-        nc.gpsimd.tensor_scalar(neg_tau[:], tau[:], -1.0, 0.0, mult, add)
         neg_tau_unscaled = column("neg_tau_unscaled")
         nc.gpsimd.tensor_scalar(neg_tau_unscaled[:], tau[:], -1.0 / OUT_SCALE, 0.0, mult, add)
 
-        query_mx = quantise("query", interleave("query_bf", query_raw))
+        (query_mx,) = quantise("query", interleave("query_bf", [query_raw]))
         size_rows = sb.tile([P, I], F32, name="size_rows", tag="query_raw")
         nc.sync.dma_start(out=size_rows[:], in_=size[0].partition_broadcast(P))
         key_scales = gather("key_scales", key_scale_pool, U8, "key_scales")
         a = product("a", query_mx, key_words, key_scales)
         val_words = gather("val_words", val_word_pool, U16, "key_scale_pool")
+        later_bf = interleave("later_bf", [dquery_raw, gout_raw])
         neg_max = column("neg_max")
         neg_a = sb.tile([P, I], F32, name="neg_a", tag="val_word_pool", align_bytes=64)
         nc.vector.tensor_scalar(neg_a[:], a[:], -1.0, None, mult, ALU.min, accum_out=neg_max[:])
-        x = wide("x")
+        x = wide("x", "gout_raw")
         nc.scalar.activation(out=x[:], in_=a[:], func=ACT.Exp, bias=neg_max[:], scale=1.0)
-        dquery_mx = quantise("dquery", interleave("dquery_bf", dquery_raw))
+        dquery_mx, gout_mx = quantise("later", later_bf)
         v = product("v", dquery_mx, key_words, key_scales)
-        gout_mx = quantise("gout", interleave("gout_bf", gout_raw))
         val_scales = gather("val_scales", val_scale_pool, U8, "val_word_pool")
         c0 = product("c0", gout_mx, val_words, val_scales)
         result = sb.tile([P, T], F32, name="result", tag="val_word_pool", align_bytes=64)
         nc.sync.dma_start(out=result[:], in_=base)
 
-        s = page_sum("s", x)
+        xv_and_s = sb.tile([P, I + G], F32, name="xv_and_s", tag="val_scale_pool", align_bytes=64)
+        xv, s = xv_and_s[:, :I], xv_and_s[:, I:]
+        nc.vector.tensor_reduce(out=s, in_=by_page(x), axis=AX.X, op=add)
         ln_s = pages("ln_s")
         nc.scalar.activation(out=ln_s[:], in_=s[:], func=ACT.Ln, bias=LN_FLOOR, scale=1.0)
         p = pages("p")
@@ -150,30 +154,27 @@ def tile_attend_hvtemperedpages_s_kernel(tc, query, keys_words, keys_scales, tem
         r = pages("r")
         nc.scalar.activation(out=r[:], in_=ln_s[:], func=ACT.Exp, scale=-1.0)
 
-        xv = wide("xv")
         nc.vector.tensor_tensor(xv[:], v[:], x[:], mult)
-        ts = page_sum("ts", xv)
+        ts_dsh = sb.tile([P, 2, G], F32, name="ts_dsh")
+        nc.vector.tensor_reduce(out=ts_dsh[:, 0, :], in_=by_page(xv), axis=AX.X, op=add)
         c = wide("c")
         nc.vector.tensor_tensor(c[:], c0[:], size_rows[:], mult)
         xc = wide("xc")
         nc.vector.tensor_tensor(xc[:], x[:], c[:], mult)
-        dsh = page_sum("dsh", xc)
+        dsh = ts_dsh[:, 1, :]
+        nc.vector.tensor_reduce(out=dsh, in_=by_page(xc), axis=AX.X, op=add)
 
         rz = column("rz")
         nc.vector.reciprocal(rz[:], z[:])
-        sums = sb.tile([P, 2], F32, name="sums")
-        terms_m = pages("terms_m")
-        nc.vector.scalar_tensor_tensor(terms_m[:], pr[:], neg_tau[:], dsh[:], mult, mult, accum_out=sums[:, 1:2])
-        terms_v = pages("terms_v")
-        nc.vector.scalar_tensor_tensor(terms_v[:], pr[:], neg_tau[:], ts[:], mult, mult, accum_out=sums[:, 0:1])
-        b = pages("b")
-        nc.vector.scalar_tensor_tensor(b[:], dsh[:], tau_less_1[:], r[:], mult, mult)
         w = pages("w")
         nc.vector.tensor_scalar(w[:], pr[:], rz[:], OUT_SCALE, mult, mult)
+        terms = sb.tile([P, 2, G], F32, name="terms", align_bytes=64)
+        nc.vector.scalar_tensor_tensor(terms[:], ts_dsh[:], neg_tau_unscaled[:], w[:].unsqueeze(1).to_broadcast([P, 2, G]), mult, mult)
+        av_b = sb.tile([P, 2, G], F32, name="av_b")
+        nc.vector.scalar_tensor_tensor(av_b[:], ts_dsh[:], tau_less_1[:], r[:].unsqueeze(1).to_broadcast([P, 2, G]), mult, mult)
+        av, b = av_b[:, 0, :], av_b[:, 1, :]
         shifts = sb.tile([P, 2], F32, name="shifts")
-        nc.vector.tensor_scalar(shifts[:], sums[:], rz[:], None, mult)
-        av = pages("av")
-        nc.vector.scalar_tensor_tensor(av[:], ts[:], tau_less_1[:], r[:], mult, mult)
+        nc.vector.tensor_reduce(out=shifts[:], in_=terms[:], axis=AX.X, op=add)
         wb = pages("wb")
         nc.vector.scalar_tensor_tensor(wb[:], b[:], shifts[:, 1:2], w[:], add, mult)
 
@@ -182,7 +183,7 @@ def tile_attend_hvtemperedpages_s_kernel(tc, query, keys_words, keys_scales, tem
             cols = slice(g * PAGE, (g + 1) * PAGE)
             nc.scalar.activation(out=t2[:, cols], in_=c[:, cols], func=ACT.Identity, scale=w[:, g : g + 1], bias=wb[:, g : g + 1])
 
-        xvc = wide("xvc")
+        xvc = sb.tile([P, I], F32, name="xvc", tag="terms", align_bytes=64)
         nc.vector.tensor_tensor(xvc[:], xv[:], c[:], mult)
         ad = pages("ad")
         nc.vector.tensor_tensor(ad[:], av[:], dsh[:], mult)

@@ -22,7 +22,7 @@ AX = mybir.AxisListType
 
 OUT_SCALE = 512.0
 LN_FLOOR = 2.0 ** -64
-STORE_WIDTHS = (384, 512, 512, 448, 192)
+STORE_WIDTHS = (320, 384, 384, 352, 320, 288)
 
 
 def tile_attend_hvtemperedpages_s_kernel(tc, query, keys_words, keys_scales, temper, gout, vals_words, vals_scales, size, dquery, base, offs, out):
@@ -156,59 +156,65 @@ def tile_attend_hvtemperedpages_s_kernel(tc, query, keys_words, keys_scales, tem
 
         nc.vector.tensor_tensor(xv[:], v[:], x[:], mult)
         ts_dsh = sb.tile([P, 2, G], F32, name="ts_dsh")
-        nc.vector.tensor_reduce(out=ts_dsh[:, 0, :], in_=by_page(xv), axis=AX.X, op=add)
+        ts, dsh = ts_dsh[:, 0, :], ts_dsh[:, 1, :]
+        nc.vector.tensor_reduce(out=ts, in_=by_page(xv), axis=AX.X, op=add)
         c = wide("c")
         nc.vector.tensor_tensor(c[:], c0[:], size_rows[:], mult)
         xc = wide("xc")
         nc.vector.tensor_tensor(xc[:], x[:], c[:], mult)
-        dsh = ts_dsh[:, 1, :]
         nc.vector.tensor_reduce(out=dsh, in_=by_page(xc), axis=AX.X, op=add)
 
         rz = column("rz")
         nc.vector.reciprocal(rz[:], z[:])
         w = pages("w")
         nc.vector.tensor_scalar(w[:], pr[:], rz[:], OUT_SCALE, mult, mult)
-        terms = sb.tile([P, 2, G], F32, name="terms", align_bytes=64)
-        nc.vector.scalar_tensor_tensor(terms[:], ts_dsh[:], neg_tau_unscaled[:], w[:].unsqueeze(1).to_broadcast([P, 2, G]), mult, mult)
+        beta = column("beta")
+        terms_m = pages("terms_m")
+        nc.vector.scalar_tensor_tensor(terms_m[:], w[:], neg_tau_unscaled[:], dsh[:], mult, mult, accum_out=beta[:])
         av_b = sb.tile([P, 2, G], F32, name="av_b")
-        nc.vector.scalar_tensor_tensor(av_b[:], ts_dsh[:], tau_less_1[:], r[:].unsqueeze(1).to_broadcast([P, 2, G]), mult, mult)
         av, b = av_b[:, 0, :], av_b[:, 1, :]
-        shifts = sb.tile([P, 2], F32, name="shifts")
-        nc.vector.tensor_reduce(out=shifts[:], in_=terms[:], axis=AX.X, op=add)
+        nc.vector.scalar_tensor_tensor(av_b[:], ts_dsh[:], tau_less_1[:], r[:].unsqueeze(1).to_broadcast([P, 2, G]), mult, mult)
         wb = pages("wb")
-        nc.vector.scalar_tensor_tensor(wb[:], b[:], shifts[:, 1:2], w[:], add, mult)
+        nc.vector.scalar_tensor_tensor(wb[:], b[:], beta[:], w[:], add, mult)
 
         t2 = wide("t2")
         for g in range(G):
             cols = slice(g * PAGE, (g + 1) * PAGE)
             nc.scalar.activation(out=t2[:, cols], in_=c[:, cols], func=ACT.Identity, scale=w[:, g : g + 1], bias=wb[:, g : g + 1])
 
-        xvc = sb.tile([P, I], F32, name="xvc", tag="terms", align_bytes=64)
+        alpha = column("alpha")
+        terms_v = pages("terms_v")
+        nc.vector.scalar_tensor_tensor(terms_v[:], w[:], neg_tau_unscaled[:], ts[:], mult, mult, accum_out=alpha[:])
+        xvc = wide("xvc")
         nc.vector.tensor_tensor(xvc[:], xv[:], c[:], mult)
+        tdsh = page_sum("tdsh", xvc)
         ad = pages("ad")
         nc.vector.tensor_tensor(ad[:], av[:], dsh[:], mult)
-        tdsh = page_sum("tdsh", xvc)
-        t1 = wide("t1")
-        nc.vector.scalar_tensor_tensor(by_page(t1), by_page(v), shifts[:, 0:1], spread(av), add, add)
 
+        ts_shifted = pages("ts_shifted")
+        nc.vector.scalar_tensor_tensor(ts_shifted[:], b[:], beta[:], ts[:], add, mult)
         y1 = pages("y1")
-        nc.vector.tensor_tensor(y1[:], ad[:], tdsh[:], add)
+        nc.vector.tensor_tensor(y1[:], ts_shifted[:], tdsh[:], add)
         y2 = pages("y2")
         nc.vector.scalar_tensor_tensor(y2[:], tdsh[:], tau_less_1[:], ad[:], mult, sub)
         terms_k = pages("terms_k")
-        acc = column("acc")
-        nc.vector.scalar_tensor_tensor(terms_k[:], w[:], neg_tau_unscaled[:], y1[:], mult, mult, accum_out=acc[:])
+        kappa = column("kappa")
+        nc.vector.scalar_tensor_tensor(terms_k[:], w[:], neg_tau_unscaled[:], y1[:], mult, mult, accum_out=kappa[:])
         gl = pages("gl")
         nc.vector.tensor_tensor(gl[:], y2[:], r[:], mult)
-        kappa = column("kappa")
-        nc.vector.tensor_scalar(kappa[:], shifts[:, 0:1], shifts[:, 1:2], acc[:], mult, add)
         wc = pages("wc")
         nc.vector.scalar_tensor_tensor(wc[:], gl[:], kappa[:], w[:], add, mult)
 
+        t1 = wide("t1")
         t3 = wide("t3")
-        nc.vector.tensor_tensor(t3[:], t1[:], t2[:], mult)
         t4 = wide("t4")
-        nc.vector.tensor_tensor(by_page(t4), by_page(t3), spread(wc), add)
+        halves = [slice(0, G // 2), slice(G // 2, G)]
+        for h in halves:
+            nc.vector.scalar_tensor_tensor(by_page(t1)[:, h], by_page(v)[:, h], alpha[:], spread(av)[:, h], add, add)
+        for h in halves:
+            nc.vector.tensor_tensor(by_page(t3)[:, h], by_page(t1)[:, h], by_page(t2)[:, h], mult)
+        for h in halves:
+            nc.vector.tensor_tensor(by_page(t4)[:, h], by_page(t3)[:, h], spread(wc)[:, h], add)
         nc.vector.tensor_tensor(placed[:].indirect(offsets[:]), t4[:], x[:], mult)
 
         start = 0

from contextlib import ExitStack

import concourse.mybir as mybir

D, T, I, Q, G = 512, 2048, 512, 128, 32
P = 128
PACK = 4
PAGE = I // G
FLOPS = 3 * 2 * D * Q * I

F32 = mybir.dt.float32
BF16 = mybir.dt.bfloat16
I32 = mybir.dt.int32
U32 = mybir.dt.uint32
U16 = mybir.dt.uint16
U8 = mybir.dt.uint8
FP8X4 = mybir.dt.float8_e4m3fn_x4
FP4X4 = mybir.dt.float4_e2m1fn_x4
ALU = mybir.AluOpType
ACT = mybir.ActivationFunctionType
AX = mybir.AxisListType

OUT_SCALE = 512.0
LN_FLOOR = 2.0 ** -64
STORE_WIDTHS = (320, 384, 384, 352, 320, 288)


def tile_attend_hvtemperedpages_s_kernel(tc, query, keys_words, keys_scales, temper, gout, vals_words, vals_scales, size, dquery, base, offs, out):
    nc = tc.nc
    mult, add, sub = ALU.mult, ALU.add, ALU.subtract

    with ExitStack() as ctx:
        sb = ctx.enter_context(tc.tile_pool(name="sb", bufs=1))
        ps = ctx.enter_context(tc.psum_pool(name="ps", bufs=1))

        def wide(name, tag=None):
            return sb.tile([P, I], F32, name=name, tag=tag or name)

        def pages(name, tag=None):
            return sb.tile([P, G], F32, name=name, tag=tag or name, align_bytes=64)

        def column(name):
            return sb.tile([P, 1], F32, name=name)

        def by_page(t):
            return t[:].rearrange("p (g j) -> p g j", j=PAGE)

        def spread(t):
            return t[:].unsqueeze(2).to_broadcast([P, G, PAGE])

        def load_scales(clearer, queue, name, scales):
            pool_scales = sb.tile([P, T], U8, name=name, tag=name, align_bytes=64)
            clearer.memset(pool_scales[:].bitcast(I32), 0)
            rows = scales[0].rearrange("(q r) n -> r q n", r=PACK)
            for r in range(PACK):
                queue.dma_start(out=pool_scales[r:P:32, :].bitcast(I32), in_=rows[r].bitcast(I32))
            return pool_scales

        def load_words(name, words):
            pool_words = sb.tile([P, T], U16, name=name, tag=name, align_bytes=64)
            nc.sync.dma_start(out=pool_words[:].bitcast(I32), in_=words[0].bitcast(I32))
            return pool_words

        def load_rows(name, rows, tag):
            raw = sb.tile([P, PACK, Q], F32, name=name, tag=tag)
            nc.sync.dma_start(out=raw[:], in_=rows.rearrange("(p j) w -> p j w", j=PACK))
            return raw

        def interleave(name, raws):
            grouped = sb.tile([P, len(raws) * Q, PACK], BF16, name=name, align_bytes=64)
            for n, raw in enumerate(raws):
                nc.scalar.copy(out=grouped[:, n * Q : (n + 1) * Q, :], in_=raw[:].rearrange("p j w -> p w j"))
            return grouped

        def quantise(name, grouped):
            width = grouped.shape[1]
            codes = sb.tile([P, width], U32, name=name + "_codes", align_bytes=64)
            scales = sb.tile([P, width], U8, name=name + "_scales", align_bytes=64)
            nc.vector.quantize_mx(out=codes[:].bitcast(FP8X4), scales=scales[:], in_=grouped[:].rearrange("p w j -> p (w j)"))
            return [(codes[:, n : n + Q], scales[:, n : n + Q]) for n in range(0, width, Q)]

        def gather(name, pool_tile, dtype, tag):
            picked = sb.tile([P, I], dtype, name=name, tag=tag, align_bytes=64)
            nc.vector.tensor_copy(out=picked[:], in_=pool_tile[:].indirect(offsets[:]))
            return picked

        def product(name, rows, words, scales):
            acc = ps.tile([P, I], F32, name=name)
            nc.tensor.matmul_mx(out=acc[:], lhsT=rows[0].bitcast(FP8X4), lhsT_scale=rows[1], rhs=words[:].bitcast(FP4X4), rhs_scale=scales[:], start=True, stop=True)
            return acc

        def page_sum(name, t):
            total = pages(name)
            nc.vector.tensor_reduce(out=total[:], in_=by_page(t), axis=AX.X, op=add)
            return total

        offsets = sb.tile([P, I // 16], U16, name="offsets")
        nc.sync.dma_start(offsets[:], offs)
        key_word_pool = load_words("key_word_pool", keys_words)
        key_scale_pool = load_scales(nc.vector, nc.sync, "key_scale_pool", keys_scales)
        query_raw = load_rows("query_raw", query, "query_raw")
        warm_in = sb.tile([P, 1], F32, name="warm_in", tag="dquery_raw")
        warm_bias = sb.tile([P, 1], F32, name="warm_bias", tag="val_word_pool", align_bytes=64)
        warm_scale = sb.tile([P, 1], F32, name="warm_scale", tag="val_scale_pool", align_bytes=64)
        for operand in (warm_in, warm_bias, warm_scale):
            nc.gpsimd.memset(operand[:], 0.0)
        warm_out = sb.tile([P, 1], F32, name="warm_out", tag="gout_raw")
        nc.scalar.activation(out=warm_out[:], in_=warm_in[:], func=ACT.Exp, bias=warm_bias[:], scale=warm_scale[:])
        val_word_pool = load_words("val_word_pool", vals_words)
        dquery_raw = load_rows("dquery_raw", dquery, "dquery_raw")
        gout_raw = load_rows("gout_raw", gout, "gout_raw")

        placed = sb.tile([P, T], F32, name="placed")
        nc.vector.memset(placed[:], 0.0)
        val_scale_pool = load_scales(nc.vector, nc.sync, "val_scale_pool", vals_scales)

        key_words = gather("key_words", key_word_pool, U16, "key_words")
        tau = sb.tile([P, 1], F32, name="tau", tag="key_word_pool", align_bytes=64)
        nc.sync.dma_start(out=tau[:], in_=temper)
        tau_less_1 = column("tau_less_1")
        nc.gpsimd.tensor_scalar(tau_less_1[:], tau[:], 1.0, -1.0, mult, add)
        neg_tau_unscaled = column("neg_tau_unscaled")
        nc.gpsimd.tensor_scalar(neg_tau_unscaled[:], tau[:], -1.0 / OUT_SCALE, 0.0, mult, add)

        (query_mx,) = quantise("query", interleave("query_bf", [query_raw]))
        size_rows = sb.tile([P, I], F32, name="size_rows", tag="query_raw")
        nc.sync.dma_start(out=size_rows[:], in_=size[0].partition_broadcast(P))
        key_scales = gather("key_scales", key_scale_pool, U8, "key_scales")
        a = product("a", query_mx, key_words, key_scales)
        val_words = gather("val_words", val_word_pool, U16, "key_scale_pool")
        later_bf = interleave("later_bf", [dquery_raw, gout_raw])
        neg_max = column("neg_max")
        neg_a = sb.tile([P, I], F32, name="neg_a", tag="val_word_pool", align_bytes=64)
        nc.vector.tensor_scalar(neg_a[:], a[:], -1.0, None, mult, ALU.min, accum_out=neg_max[:])
        x = wide("x", "gout_raw")
        nc.scalar.activation(out=x[:], in_=a[:], func=ACT.Exp, bias=neg_max[:], scale=1.0)
        dquery_mx, gout_mx = quantise("later", later_bf)
        v = product("v", dquery_mx, key_words, key_scales)
        val_scales = gather("val_scales", val_scale_pool, U8, "val_word_pool")
        c0 = product("c0", gout_mx, val_words, val_scales)
        result = sb.tile([P, T], F32, name="result", tag="val_word_pool", align_bytes=64)
        nc.sync.dma_start(out=result[:], in_=base)

        xv_and_s = sb.tile([P, I + G], F32, name="xv_and_s", tag="val_scale_pool", align_bytes=64)
        xv, s = xv_and_s[:, :I], xv_and_s[:, I:]
        nc.vector.tensor_reduce(out=s, in_=by_page(x), axis=AX.X, op=add)
        ln_s = pages("ln_s")
        nc.scalar.activation(out=ln_s[:], in_=s[:], func=ACT.Ln, bias=LN_FLOOR, scale=1.0)
        p = pages("p")
        z = column("z")
        nc.scalar.activation(out=p[:], in_=ln_s[:], func=ACT.Exp, scale=tau[:], accum_out=z[:])
        pr = pages("pr")
        nc.scalar.activation(out=pr[:], in_=ln_s[:], func=ACT.Exp, scale=tau_less_1[:])
        r = pages("r")
        nc.scalar.activation(out=r[:], in_=ln_s[:], func=ACT.Exp, scale=-1.0)

        nc.vector.tensor_tensor(xv[:], v[:], x[:], mult)
        ts_dsh = sb.tile([P, 2, G], F32, name="ts_dsh")
        ts, dsh = ts_dsh[:, 0, :], ts_dsh[:, 1, :]
        nc.vector.tensor_reduce(out=ts, in_=by_page(xv), axis=AX.X, op=add)
        c = wide("c")
        nc.vector.tensor_tensor(c[:], c0[:], size_rows[:], mult)
        xc = wide("xc")
        nc.vector.tensor_tensor(xc[:], x[:], c[:], mult)
        nc.vector.tensor_reduce(out=dsh, in_=by_page(xc), axis=AX.X, op=add)

        rz = column("rz")
        nc.vector.reciprocal(rz[:], z[:])
        w = pages("w")
        nc.vector.tensor_scalar(w[:], pr[:], rz[:], OUT_SCALE, mult, mult)
        beta = column("beta")
        terms_m = pages("terms_m")
        nc.vector.scalar_tensor_tensor(terms_m[:], w[:], neg_tau_unscaled[:], dsh[:], mult, mult, accum_out=beta[:])
        av_b = sb.tile([P, 2, G], F32, name="av_b")
        av, b = av_b[:, 0, :], av_b[:, 1, :]
        nc.vector.scalar_tensor_tensor(av_b[:], ts_dsh[:], tau_less_1[:], r[:].unsqueeze(1).to_broadcast([P, 2, G]), mult, mult)
        wb = pages("wb")
        nc.vector.scalar_tensor_tensor(wb[:], b[:], beta[:], w[:], add, mult)

        t2 = wide("t2")
        for g in range(G):
            cols = slice(g * PAGE, (g + 1) * PAGE)
            nc.scalar.activation(out=t2[:, cols], in_=c[:, cols], func=ACT.Identity, scale=w[:, g : g + 1], bias=wb[:, g : g + 1])

        alpha = column("alpha")
        terms_v = pages("terms_v")
        nc.vector.scalar_tensor_tensor(terms_v[:], w[:], neg_tau_unscaled[:], ts[:], mult, mult, accum_out=alpha[:])
        xvc = wide("xvc")
        nc.vector.tensor_tensor(xvc[:], xv[:], c[:], mult)
        tdsh = page_sum("tdsh", xvc)
        ad = pages("ad")
        nc.vector.tensor_tensor(ad[:], av[:], dsh[:], mult)

        ts_shifted = pages("ts_shifted")
        nc.vector.scalar_tensor_tensor(ts_shifted[:], b[:], beta[:], ts[:], add, mult)
        y1 = pages("y1")
        nc.vector.tensor_tensor(y1[:], ts_shifted[:], tdsh[:], add)
        y2 = pages("y2")
        nc.vector.scalar_tensor_tensor(y2[:], tdsh[:], tau_less_1[:], ad[:], mult, sub)
        terms_k = pages("terms_k")
        kappa = column("kappa")
        nc.vector.scalar_tensor_tensor(terms_k[:], w[:], neg_tau_unscaled[:], y1[:], mult, mult, accum_out=kappa[:])
        gl = pages("gl")
        nc.vector.tensor_tensor(gl[:], y2[:], r[:], mult)
        wc = pages("wc")
        nc.vector.scalar_tensor_tensor(wc[:], gl[:], kappa[:], w[:], add, mult)

        t1 = wide("t1")
        t3 = wide("t3")
        t4 = wide("t4")
        halves = [slice(0, G // 2), slice(G // 2, G)]
        for h in halves:
            nc.vector.scalar_tensor_tensor(by_page(t1)[:, h], by_page(v)[:, h], alpha[:], spread(av)[:, h], add, add)
        for h in halves:
            nc.vector.tensor_tensor(by_page(t3)[:, h], by_page(t1)[:, h], by_page(t2)[:, h], mult)
        for h in halves:
            nc.vector.tensor_tensor(by_page(t4)[:, h], by_page(t3)[:, h], spread(wc)[:, h], add)
        nc.vector.tensor_tensor(placed[:].indirect(offsets[:]), t4[:], x[:], mult)

        start = 0
        for n, width in enumerate(STORE_WIDTHS):
            cols = slice(start, start + width)
            nc.vector.tensor_tensor(result[:, cols], result[:, cols], placed[:, cols], add)
            (nc.sync if n % 2 == 0 else nc.scalar).dma_start(out=out[:, cols], in_=result[:, cols])
            start += width
